import numpy as np
import ml_dtypes

BF16 = ml_dtypes.bfloat16


def bf(x):
    return np.asarray(x, np.float32).astype(BF16)


def f32(x):
    return np.asarray(x, np.float32)


def f64(x):
    return np.asarray(x).astype(np.float64)


def striped(idx):
    return np.tile(idx.reshape(-1, 16).T, (8, 1))


S, K, M, N = 256, 128, 128, 256


def setup_inputs():
    return {"base": bf(np.random.standard_normal((M, S))), "x": bf(np.random.standard_normal((K, N))), "w": bf(np.random.standard_normal((K, M)) / np.sqrt(K)), "offs": striped(np.random.permutation(S))}


def reference(base, x, w, offs):
    idx = offs[:16].T.reshape(-1)
    z = f64(base).copy()
    z[:, idx] += f64(w).T @ f64(x)
    return z

@@ -1,0 +1,39 @@
+import concourse.mybir as mybir
+from concourse.masks import make_identity
+
+BF16, F32, U16 = mybir.dt.bfloat16, mybir.dt.float32, mybir.dt.uint16
+
+P = 128
+S = 256
+N = 256
+
+FLOPS = 2 * P * P * N
+
+
+def tile_scatter_matmul_kernel(tc, base, x, w, offs, out):
+    nc = tc.nc
+    with (
+        tc.tile_pool(name="held", bufs=1) as held,
+        tc.psum_pool(name="psum", bufs=1) as psum,
+    ):
+        offsets = held.tile([P, N // 16], U16, name="offsets")
+        nc.sync.dma_start(offsets[:], offs)
+
+        base_tile = held.tile([P, S], BF16, name="base_tile")
+        nc.scalar.dma_start(base_tile[:], base)
+        x_tile = held.tile([P, N], BF16, name="x_tile")
+        nc.sync.dma_start(x_tile[:], x)
+        w_tile = held.tile([P, P], BF16, name="w_tile")
+        nc.scalar.dma_start(w_tile[:], w)
+
+        ident = held.tile([P, P], BF16, name="ident")
+        make_identity(nc, ident[:])
+
+        window = psum.tile([P, S], F32, name="window")
+        nc.tensor.matmul(window[:], ident[:], base_tile[:], start=True, stop=False)
+
+        nc.tensor.matmul(window[:].indirect(offsets[:]), w_tile[:], x_tile[:], start=False, stop=True)
+
+        z_tile = held.tile([P, S], F32, name="z_tile")
+        nc.vector.tensor_copy(z_tile[:], window[:])
+        nc.sync.dma_start(out, z_tile[:])

@@ -35,5 +35,8 @@ def tile_scatter_matmul_kernel(tc, base, x, w, offs, out):
         nc.tensor.matmul(window[:].indirect(offsets[:]), w_tile[:], x_tile[:], start=False, stop=True)
 
         z_tile = held.tile([P, S], F32, name="z_tile")
-        nc.vector.tensor_copy(z_tile[:], window[:])
-        nc.sync.dma_start(out, z_tile[:])
+        half = S // 2
+        for h, queue in enumerate((nc.sync, nc.scalar)):
+            columns = slice(h * half, (h + 1) * half)
+            nc.vector.tensor_copy(z_tile[:, columns], window[:, columns])
+            queue.dma_start(out[:, columns], z_tile[:, columns])

@@ -16,15 +16,14 @@ def tile_scatter_matmul_kernel(tc, base, x, w, offs, out):
         tc.tile_pool(name="held", bufs=1) as held,
         tc.psum_pool(name="psum", bufs=1) as psum,
     ):
-        offsets = held.tile([P, N // 16], U16, name="offsets")
-        nc.sync.dma_start(offsets[:], offs)
-
         base_tile = held.tile([P, S], BF16, name="base_tile")
-        nc.scalar.dma_start(base_tile[:], base)
+        nc.sync.dma_start(base_tile[:], base)
         x_tile = held.tile([P, N], BF16, name="x_tile")
         nc.sync.dma_start(x_tile[:], x)
         w_tile = held.tile([P, P], BF16, name="w_tile")
-        nc.scalar.dma_start(w_tile[:], w)
+        nc.sync.dma_start(w_tile[:], w)
+        offsets = held.tile([P, N // 16], U16, name="offsets")
+        nc.sync.dma_start(offsets[:], offs)
 
         ident = held.tile([P, P], BF16, name="ident")
         make_identity(nc, ident[:])
@@ -35,8 +34,5 @@ def tile_scatter_matmul_kernel(tc, base, x, w, offs, out):
         nc.tensor.matmul(window[:].indirect(offsets[:]), w_tile[:], x_tile[:], start=False, stop=True)
 
         z_tile = held.tile([P, S], F32, name="z_tile")
-        half = S // 2
-        for h, queue in enumerate((nc.sync, nc.scalar)):
-            columns = slice(h * half, (h + 1) * half)
-            nc.vector.tensor_copy(z_tile[:, columns], window[:, columns])
-            queue.dma_start(out[:, columns], z_tile[:, columns])
+        nc.vector.tensor_copy(z_tile[:], window[:])
+        nc.sync.dma_start(out, z_tile[:])

@@ -7,6 +7,9 @@ P = 128
 S = 256
 N = 256
 
+STRIP = 32
+WARM_UP_ROUNDS = 4
+
 FLOPS = 2 * P * P * N
 
 
@@ -27,6 +30,15 @@ def tile_scatter_matmul_kernel(tc, base, x, w, offs, out):
 
         ident = held.tile([P, P], BF16, name="ident")
         make_identity(nc, ident[:])
+
+        zeros = held.tile([P, N], BF16, name="zeros")
+        nc.vector.memset(zeros[:], 0.0)
+        unread = psum.tile([P, N], F32, name="unread")
+        for _ in range(WARM_UP_ROUNDS):
+            for q in range(P // STRIP):
+                nc.tensor.matmul(
+                    unread[q * STRIP : (q + 1) * STRIP, :], zeros[:, :STRIP], zeros[:], start=True, stop=True
+                )
 
         window = psum.tile([P, S], F32, name="window")
         nc.tensor.matmul(window[:], ident[:], base_tile[:], start=True, stop=False)

@@ -39,6 +39,7 @@ def tile_scatter_matmul_kernel(tc, base, x, w, offs, out):
                 nc.tensor.matmul(
                     unread[q * STRIP : (q + 1) * STRIP, :], zeros[:, :STRIP], zeros[:], start=True, stop=True
                 )
+        nc.tensor.matmul(unread[:, :P], zeros[:, :P], zeros[:, :P], start=True, stop=True)
 
         window = psum.tile([P, S], F32, name="window")
         nc.tensor.matmul(window[:], ident[:], base_tile[:], start=True, stop=False)
@@ -46,5 +47,7 @@ def tile_scatter_matmul_kernel(tc, base, x, w, offs, out):
         nc.tensor.matmul(window[:].indirect(offsets[:]), w_tile[:], x_tile[:], start=False, stop=True)
 
         z_tile = held.tile([P, S], F32, name="z_tile")
-        nc.vector.tensor_copy(z_tile[:], window[:])
-        nc.sync.dma_start(out, z_tile[:])
+        for h in range(2):
+            half = slice(h * (S // 2), (h + 1) * (S // 2))
+            nc.vector.tensor_copy(z_tile[:, half], window[:, half])
+            nc.sync.dma_start(out[:, half], z_tile[:, half])

@@ -8,7 +8,8 @@ S = 256
 N = 256
 
 STRIP = 32
-WARM_UP_ROUNDS = 4
+REPEATS = N // STRIP
+WARM_UP_ROUNDS = 5
 
 FLOPS = 2 * P * P * N
 
@@ -28,18 +29,21 @@ def tile_scatter_matmul_kernel(tc, base, x, w, offs, out):
         offsets = held.tile([P, N // 16], U16, name="offsets")
         nc.sync.dma_start(offsets[:], offs)
 
-        ident = held.tile([P, P], BF16, name="ident")
-        make_identity(nc, ident[:])
-
-        zeros = held.tile([P, N], BF16, name="zeros")
+        zeros = held.tile([P, STRIP], BF16, name="zeros")
         nc.vector.memset(zeros[:], 0.0)
-        unread = psum.tile([P, N], F32, name="unread")
+
+        ident = held.tile([P, P], BF16, name="ident")
+        nc.vector.memset(ident[:], 0.0)
+        make_identity(nc, ident[:], nomemset=True)
+
+        zeros_repeated = zeros[:].unsqueeze(1).to_broadcast([P, REPEATS, STRIP])
+        unread = psum.tile([P, REPEATS, STRIP], F32, name="unread")
         for _ in range(WARM_UP_ROUNDS):
             for q in range(P // STRIP):
                 nc.tensor.matmul(
-                    unread[q * STRIP : (q + 1) * STRIP, :], zeros[:, :STRIP], zeros[:], start=True, stop=True
+                    unread[q * STRIP : (q + 1) * STRIP, :, :], zeros[:], zeros_repeated, start=True, stop=True
                 )
-        nc.tensor.matmul(unread[:, :P], zeros[:, :P], zeros[:, :P], start=True, stop=True)
+        nc.tensor.matmul(unread[:, 0, :], ident[:], zeros[:], start=True, stop=True)
 
         window = psum.tile([P, S], F32, name="window")
         nc.tensor.matmul(window[:], ident[:], base_tile[:], start=True, stop=False)

@@ -23,11 +23,11 @@ def tile_scatter_matmul_kernel(tc, base, x, w, offs, out):
         base_tile = held.tile([P, S], BF16, name="base_tile")
         nc.sync.dma_start(base_tile[:], base)
         x_tile = held.tile([P, N], BF16, name="x_tile")
-        nc.sync.dma_start(x_tile[:], x)
-        w_tile = held.tile([P, P], BF16, name="w_tile")
-        nc.sync.dma_start(w_tile[:], w)
+        nc.scalar.dma_start(x_tile[:], x)
         offsets = held.tile([P, N // 16], U16, name="offsets")
         nc.sync.dma_start(offsets[:], offs)
+        w_tile = held.tile([P, P], BF16, name="w_tile")
+        nc.scalar.dma_start(w_tile[:], w)
 
         zeros = held.tile([P, STRIP], BF16, name="zeros")
         nc.vector.memset(zeros[:], 0.0)

@@ -7,10 +7,6 @@ P = 128
 S = 256
 N = 256
 
-STRIP = 32
-REPEATS = N // STRIP
-WARM_UP_ROUNDS = 5
-
 FLOPS = 2 * P * P * N
 
 
@@ -29,21 +25,9 @@ def tile_scatter_matmul_kernel(tc, base, x, w, offs, out):
         w_tile = held.tile([P, P], BF16, name="w_tile")
         nc.scalar.dma_start(w_tile[:], w)
 
-        zeros = held.tile([P, STRIP], BF16, name="zeros")
-        nc.vector.memset(zeros[:], 0.0)
-
         ident = held.tile([P, P], BF16, name="ident")
         nc.vector.memset(ident[:], 0.0)
         make_identity(nc, ident[:], nomemset=True)
-
-        zeros_repeated = zeros[:].unsqueeze(1).to_broadcast([P, REPEATS, STRIP])
-        unread = psum.tile([P, REPEATS, STRIP], F32, name="unread")
-        for _ in range(WARM_UP_ROUNDS):
-            for q in range(P // STRIP):
-                nc.tensor.matmul(
-                    unread[q * STRIP : (q + 1) * STRIP, :, :], zeros[:], zeros_repeated, start=True, stop=True
-                )
-        nc.tensor.matmul(unread[:, 0, :], ident[:], zeros[:], start=True, stop=True)
 
         window = psum.tile([P, S], F32, name="window")
         nc.tensor.matmul(window[:], ident[:], base_tile[:], start=True, stop=False)

@@ -7,6 +7,8 @@ P = 128
 S = 256
 N = 256
 
+FIRST = 64
+
 FLOPS = 2 * P * P * N
 
 
@@ -35,7 +37,6 @@ def tile_scatter_matmul_kernel(tc, base, x, w, offs, out):
         nc.tensor.matmul(window[:].indirect(offsets[:]), w_tile[:], x_tile[:], start=False, stop=True)
 
         z_tile = held.tile([P, S], F32, name="z_tile")
-        for h in range(2):
-            half = slice(h * (S // 2), (h + 1) * (S // 2))
-            nc.vector.tensor_copy(z_tile[:, half], window[:, half])
-            nc.sync.dma_start(out[:, half], z_tile[:, half])
+        for piece in (slice(0, FIRST), slice(FIRST, S)):
+            nc.vector.tensor_copy(z_tile[:, piece], window[:, piece])
+            nc.sync.dma_start(out[:, piece], z_tile[:, piece])

@@ -7,6 +7,7 @@ P = 128
 S = 256
 N = 256
 
+ROW_ALIGN = 256
 FIRST = 64
 
 FLOPS = 2 * P * P * N
@@ -18,13 +19,13 @@ def tile_scatter_matmul_kernel(tc, base, x, w, offs, out):
         tc.tile_pool(name="held", bufs=1) as held,
         tc.psum_pool(name="psum", bufs=1) as psum,
     ):
-        base_tile = held.tile([P, S], BF16, name="base_tile")
+        base_tile = held.tile([P, S], BF16, name="base_tile", align_bytes=ROW_ALIGN)
         nc.sync.dma_start(base_tile[:], base)
-        x_tile = held.tile([P, N], BF16, name="x_tile")
+        x_tile = held.tile([P, N], BF16, name="x_tile", align_bytes=ROW_ALIGN)
         nc.scalar.dma_start(x_tile[:], x)
         offsets = held.tile([P, N // 16], U16, name="offsets")
         nc.sync.dma_start(offsets[:], offs)
-        w_tile = held.tile([P, P], BF16, name="w_tile")
+        w_tile = held.tile([P, P], BF16, name="w_tile", align_bytes=ROW_ALIGN)
         nc.scalar.dma_start(w_tile[:], w)
 
         ident = held.tile([P, P], BF16, name="ident")
@@ -36,7 +37,7 @@ def tile_scatter_matmul_kernel(tc, base, x, w, offs, out):
 
         nc.tensor.matmul(window[:].indirect(offsets[:]), w_tile[:], x_tile[:], start=False, stop=True)
 
-        z_tile = held.tile([P, S], F32, name="z_tile")
+        z_tile = held.tile([P, S], F32, name="z_tile", align_bytes=ROW_ALIGN)
         for piece in (slice(0, FIRST), slice(FIRST, S)):
             nc.vector.tensor_copy(z_tile[:, piece], window[:, piece])
             nc.sync.dma_start(out[:, piece], z_tile[:, piece])

@@ -8,6 +8,7 @@ S = 256
 N = 256
 
 ROW_ALIGN = 256
+WARM_UPS = 5
 FIRST = 64
 
 FLOPS = 2 * P * P * N
@@ -28,9 +29,18 @@ def tile_scatter_matmul_kernel(tc, base, x, w, offs, out):
         w_tile = held.tile([P, P], BF16, name="w_tile", align_bytes=ROW_ALIGN)
         nc.scalar.dma_start(w_tile[:], w)
 
+        zeros = held.tile([P, 1], BF16, name="zeros")
+        nc.vector.memset(zeros[:], 0.0)
+
         ident = held.tile([P, P], BF16, name="ident")
         nc.vector.memset(ident[:], 0.0)
         make_identity(nc, ident[:], nomemset=True)
+
+        unread = psum.tile([P, S], F32, name="unread")
+        for _ in range(WARM_UPS):
+            nc.tensor.matmul(
+                unread[:], zeros[:].to_broadcast([P, P]), zeros[:].to_broadcast([P, S]), start=True, stop=True
+            )
 
         window = psum.tile([P, S], F32, name="window")
         nc.tensor.matmul(window[:], ident[:], base_tile[:], start=True, stop=False)

@@ -7,7 +7,7 @@ P = 128
 S = 256
 N = 256
 
-ROW_ALIGN = 256
+BF16_BYTES, F32_BYTES = 2, 4
 WARM_UPS = 5
 FIRST = 64
 
@@ -20,13 +20,13 @@ def tile_scatter_matmul_kernel(tc, base, x, w, offs, out):
         tc.tile_pool(name="held", bufs=1) as held,
         tc.psum_pool(name="psum", bufs=1) as psum,
     ):
-        base_tile = held.tile([P, S], BF16, name="base_tile", align_bytes=ROW_ALIGN)
+        base_tile = held.tile([P, S], BF16, name="base_tile", align_bytes=S * BF16_BYTES)
         nc.sync.dma_start(base_tile[:], base)
-        x_tile = held.tile([P, N], BF16, name="x_tile", align_bytes=ROW_ALIGN)
+        x_tile = held.tile([P, N], BF16, name="x_tile", align_bytes=N * BF16_BYTES)
         nc.scalar.dma_start(x_tile[:], x)
         offsets = held.tile([P, N // 16], U16, name="offsets")
         nc.sync.dma_start(offsets[:], offs)
-        w_tile = held.tile([P, P], BF16, name="w_tile", align_bytes=ROW_ALIGN)
+        w_tile = held.tile([P, P], BF16, name="w_tile", align_bytes=P * BF16_BYTES)
         nc.scalar.dma_start(w_tile[:], w)
 
         zeros = held.tile([P, 1], BF16, name="zeros")
@@ -47,7 +47,7 @@ def tile_scatter_matmul_kernel(tc, base, x, w, offs, out):
 
         nc.tensor.matmul(window[:].indirect(offsets[:]), w_tile[:], x_tile[:], start=False, stop=True)
 
-        z_tile = held.tile([P, S], F32, name="z_tile", align_bytes=ROW_ALIGN)
+        z_tile = held.tile([P, S], F32, name="z_tile", align_bytes=S * F32_BYTES)
         for piece in (slice(0, FIRST), slice(FIRST, S)):
             nc.vector.tensor_copy(z_tile[:, piece], window[:, piece])
             nc.sync.dma_start(out[:, piece], z_tile[:, piece])

@@ -8,7 +8,6 @@ S = 256
 N = 256
 
 BF16_BYTES, F32_BYTES = 2, 4
-WARM_UPS = 5
 FIRST = 64
 
 FLOPS = 2 * P * P * N
@@ -29,18 +28,9 @@ def tile_scatter_matmul_kernel(tc, base, x, w, offs, out):
         w_tile = held.tile([P, P], BF16, name="w_tile", align_bytes=P * BF16_BYTES)
         nc.scalar.dma_start(w_tile[:], w)
 
-        zeros = held.tile([P, 1], BF16, name="zeros")
-        nc.vector.memset(zeros[:], 0.0)
-
         ident = held.tile([P, P], BF16, name="ident")
         nc.vector.memset(ident[:], 0.0)
         make_identity(nc, ident[:], nomemset=True)
-
-        unread = psum.tile([P, S], F32, name="unread")
-        for _ in range(WARM_UPS):
-            nc.tensor.matmul(
-                unread[:], zeros[:].to_broadcast([P, P]), zeros[:].to_broadcast([P, S]), start=True, stop=True
-            )
 
         window = psum.tile([P, S], F32, name="window")
         nc.tensor.matmul(window[:], ident[:], base_tile[:], start=True, stop=False)

import concourse.mybir as mybir
from concourse.masks import make_identity

BF16, F32, U16 = mybir.dt.bfloat16, mybir.dt.float32, mybir.dt.uint16

P = 128
S = 256
N = 256

BF16_BYTES, F32_BYTES = 2, 4
FIRST = 64

FLOPS = 2 * P * P * N


def tile_scatter_matmul_kernel(tc, base, x, w, offs, out):
    nc = tc.nc
    with (
        tc.tile_pool(name="held", bufs=1) as held,
        tc.psum_pool(name="psum", bufs=1) as psum,
    ):
        base_tile = held.tile([P, S], BF16, name="base_tile", align_bytes=S * BF16_BYTES)
        nc.sync.dma_start(base_tile[:], base)
        x_tile = held.tile([P, N], BF16, name="x_tile", align_bytes=N * BF16_BYTES)
        nc.scalar.dma_start(x_tile[:], x)
        offsets = held.tile([P, N // 16], U16, name="offsets")
        nc.sync.dma_start(offsets[:], offs)
        w_tile = held.tile([P, P], BF16, name="w_tile", align_bytes=P * BF16_BYTES)
        nc.scalar.dma_start(w_tile[:], w)

        ident = held.tile([P, P], BF16, name="ident")
        nc.vector.memset(ident[:], 0.0)
        make_identity(nc, ident[:], nomemset=True)

        window = psum.tile([P, S], F32, name="window")
        nc.tensor.matmul(window[:], ident[:], base_tile[:], start=True, stop=False)

        nc.tensor.matmul(window[:].indirect(offsets[:]), w_tile[:], x_tile[:], start=False, stop=True)

        z_tile = held.tile([P, S], F32, name="z_tile", align_bytes=S * F32_BYTES)
        for piece in (slice(0, FIRST), slice(FIRST, S)):
            nc.vector.tensor_copy(z_tile[:, piece], window[:, piece])
            nc.sync.dma_start(out[:, piece], z_tile[:, piece])
